import numpy as np, ml_dtypes
CORES = [89,94,345,350]
N = 4
import mx_ref
NC = 128
BF = ml_dtypes.bfloat16
def cut(t, i, w=512):
    return t[:, w * i:w * i + w]
def term(a, B):
    return np.stack([np.maximum(mx_ref.matmul(mx_ref.quantize(cut(a, i)), B), 0) for i in range(4)], axis=2).reshape(128, -1)
def setup_inputs(rng):
    def f(*shape):
        return mx_ref.flush((rng.standard_normal(shape, dtype=np.float32) * np.exp2(rng.integers(-2, 3, shape[:-1] + (1,)))).astype(BF))
    return {"a": f(N, 128, 4 * 512), "b": f(N, 128, 4 * NC)}
def setup_inputs_blocks(rng):
    d = setup_inputs(rng)
    for k in ("a", "b"): d[k] = mx_ref.spread(d[k], rng, 2)
    return d
def setup_inputs_wide(rng):
    d = setup_inputs(rng)
    for k in ("a", "b"): d[k] = mx_ref.flush((d[k].astype(np.float32) * np.exp2(rng.integers(-4, 5, (N, 1, 1))).astype(np.float32)).astype(BF))
    return d
def setup_inputs_lossless(rng):
    a = np.zeros((N, 128, 4 * 128, 4), np.float32)
    for r in range(N):
        k = rng.integers(0, 512, size=4 * 128)
        a[r, k // 4, np.arange(4 * 128), k % 4] = 1.0
    size = np.repeat(2.0 ** rng.integers(-4, 5, size=(1, 1, (4 * NC) // 4)), 4, axis=2)
    b = (rng.random((N, 128, 4 * NC)) < 0.8) * size
    return {"a": a.reshape(N, 128, 4 * 512).astype(BF), "b": b.astype(np.float32).astype(BF)}
def reference(a, b):
    Bq = [mx_ref.quantize(b[c]) for c in range(N)]
    y = np.zeros((N, 128, 4 * NC), np.float32)
    for c in range(N):
        y[c] = mx_ref.total([term(a[r], Bq[c]) for r in range(N)])
    return {"y": y}

@@ -1,0 +1,210 @@
+from concourse.mybir import dt, AluOpType, ActivationFunctionType
+
+CODES = "float8_e4m3fn_x4"
+W = 512
+NC = 128
+TILES = 4
+SIM_CORES = 512
+
+SCRATCH = {
+    "bbf": ("sbuf", [128, W], "bfloat16"),
+    "abf": ("sbuf", [128, TILES * W], "bfloat16"),
+    "bq": ("sbuf", [128, NC], CODES),
+    "bs": ("sbuf", [128, NC], "uint8"),
+    "aq": ("sbuf", [128, TILES * NC], CODES),
+    "asc": ("sbuf", [128, TILES * NC], "uint8"),
+    "noq": ("sbuf", [128, TILES * NC], CODES),
+    "nos": ("sbuf", [128, TILES * NC], "uint8"),
+    "wq": ("sbuf", [128, TILES * NC], CODES),
+    "ws": ("sbuf", [128, TILES * NC], "uint8"),
+    "m0q": ("sbuf", [128, NC], CODES),
+    "m0s": ("sbuf", [128, NC], "uint8"),
+    "m1q": ("sbuf", [128, NC], CODES),
+    "m1s": ("sbuf", [128, NC], "uint8"),
+    "h0": ("sbuf", [128, W], "bfloat16"),
+    "h1": ("sbuf", [128, W], "bfloat16"),
+    "h0q": ("sbuf", [128, NC], CODES),
+    "h0s": ("sbuf", [128, NC], "uint8"),
+    "h1q": ("sbuf", [128, NC], CODES),
+    "h1s": ("sbuf", [128, NC], "uint8"),
+    "t0q": ("sbuf", [128, NC], CODES),
+    "t0s": ("sbuf", [128, NC], "uint8"),
+    "t1q": ("sbuf", [128, NC], CODES),
+    "t1s": ("sbuf", [128, NC], "uint8"),
+    "ones": ("sbuf", [128, W], "bfloat16"),
+    "sel": ("sbuf", [128, TILES * W], "bfloat16"),
+    "selq": ("sbuf", [128, TILES * NC], CODES),
+    "sels": ("sbuf", [128, TILES * NC], "uint8"),
+    "own": ("sbuf", [128, W], "float32"),
+    "nei": ("sbuf", [128, W], "float32"),
+    "near": ("sbuf", [128, W], "float32"),
+    "yo": ("sbuf", [128, W], "float32"),
+    "ps": ("psum", [128, 512 * 8], "float32"),
+}
+SEMAPHORES = ["lb", "la0", "la1", "ones", "qb", "qa", "sel", "qsel", "pe", "pu", "act", "vec", "near", "vy", "sty",
+              "nin", "win", "m0c", "m0p", "m1in", "qh", "t0in", "t1in", "sent"]
+
+RELU = ActivationFunctionType.Relu
+_PLAN = {}
+
+
+def _plan(T, topo):
+    if _PLAN:
+        return _PLAN
+    sides = []
+    for c in T.cores:
+        if topo.host(c) not in sides:
+            sides.append(topo.host(c))
+
+    def place(c):
+        return sum(1 for d in range(c) if topo.host(d) == topo.host(c) and topo.chip(d) == topo.chip(c))
+
+    ranks, helpers = {}, {}
+    for s, h in enumerate(sides):
+        for k, c in enumerate([c for c in T.cores if topo.host(c) == h]):
+            ranks[s, k] = c
+            other = sides[1 - s]
+            for d in range(SIM_CORES):
+                if (topo.host(d) not in sides and topo.chip(d) == topo.chip(c)
+                        and topo.rack(topo.host(d)) == topo.rack(other) and place(d) == place(c)):
+                    helpers[s, k] = d
+    _PLAN.update({"rank": ranks, "helper": helpers,
+                  "role": dict([(c, ("rank",) + sk) for sk, c in ranks.items()]
+                               + [(c, ("helper",) + sk) for sk, c in helpers.items()])})
+    return _PLAN
+
+
+def _u8(view):
+    return view.bitcast(dt.uint8)
+
+
+def _engines(mask):
+    return bin(mask).count("1")
+
+
+def rank_program(g, core, T, topo):
+    plan = _plan(T, topo)
+    role = plan["role"].get(core)
+    if role is None:
+        return
+    sent = [0]
+
+    def send(dst, out, in_, sem, mask):
+        rid, pid = topo.addr(dst, core)
+        g.remote_dma(out, in_, sem, T.sem.sent, pid, rid, mask)
+        sent[0] += _engines(mask)
+
+    def bank(k):
+        return T.ps[:, 512 * k:512 * k + NC]
+
+    def tile(buf, i):
+        return buf[:, NC * i:NC * i + NC]
+
+    kind, s, k = role
+    ranks, helpers = plan["rank"], plan["helper"]
+    off = topo.mask(ranks[s, k], helpers[s, k])
+    ne = _engines(off)
+
+    if kind == "rank":
+        mate = ranks[s, 1 - k]
+        mine = helpers[s, k]
+        far = helpers[1 - s, k]
+        onchip = topo.mask(core, mate) & ~off
+        nn = _engines(onchip)
+
+        g.sync.dma_start(T.bbf[:], T.b[:]).then_inc(T.sem.lb, 16)
+        g.scalar.dma_start(T.abf[:, 0:2 * W], T.a[:, 0:2 * W]).then_inc(T.sem.la0, 16)
+        g.sync.dma_start(T.abf[:, 2 * W:4 * W], T.a[:, 2 * W:4 * W]).then_inc(T.sem.la1, 16)
+
+        v = g.vector
+        v.memset(T.ones[:], 1.0).then_inc(T.sem.ones, 1)
+        v.wait_ge(T.sem.lb, 16)
+        v.quantize_mx(T.bq[:], T.bs[:], T.bbf[:]).then_inc(T.sem.qb, 1)
+        for h in range(2):
+            v.wait_ge(T.sem["la%d" % h], 16)
+            v.quantize_mx(T.aq[:, 2 * NC * h:2 * NC * (h + 1)], T.asc[:, 2 * NC * h:2 * NC * (h + 1)],
+                          T.abf[:, 2 * W * h:2 * W * (h + 1)]).then_inc(T.sem.qa, 1)
+
+        g.wait_ge(T.sem.qb, 1)
+        send(mine, _u8(T.m0q[:]), _u8(T.bq[:]), T.sem.m0c, off)
+        send(mine, T.m0s[:], T.bs[:], T.sem.m0p, off)
+        g.wait_ge(T.sem.qa, 2)
+        send(far, _u8(T.wq[:]), _u8(T.aq[:]), T.sem.win, off)
+        send(far, T.ws[:], T.asc[:], T.sem.win, off)
+        send(mate, _u8(T.noq[:]), _u8(T.aq[:]), T.sem.nin, onchip)
+        send(mate, T.nos[:], T.asc[:], T.sem.nin, onchip)
+        g.wait_ge(T.sem.ones, 1)
+        for i in range(TILES):
+            g.affine_select(T.sel[:, W * i:W * i + W], T.ones[:], [[1, W]], AluOpType.is_equal, 0.0, -i,
+                            -4).then_inc(T.sem.sel, 1)
+        for i in range(TILES):
+            v.wait_ge(T.sem.sel, i + 1)
+            v.quantize_mx(tile(T.selq, i), tile(T.sels, i), T.sel[:, W * i:W * i + W]).then_inc(T.sem.qsel, 1)
+
+        p = g.tensor
+        p.wait_ge(T.sem.qb, 1)
+        p.wait_ge(T.sem.qa, 2)
+        for i in range(TILES):
+            p.matmul_mx(bank(i), tile(T.aq, i), tile(T.asc, i), T.bq[:], T.bs[:], True, True).then_inc(T.sem.pe, 1)
+        p.wait_ge(T.sem.nin, 2 * nn)
+        for i in range(TILES):
+            p.matmul_mx(bank(4 + i), tile(T.noq, i), tile(T.nos, i), T.bq[:], T.bs[:], True, True).then_inc(T.sem.pe, 1)
+        for j in range(2 * TILES):
+            g.scalar.wait_ge(T.sem.pe, j + 1)
+            dst = T.own if j < TILES else T.nei
+            i = j % TILES
+            g.scalar.activation(dst[:, i:W:4], bank(j), RELU).then_inc(T.sem.act, 1)
+        v.wait_ge(T.sem.act, 2 * TILES)
+        v.tensor_tensor(T.near[:], T.own[:], T.nei[:], AluOpType.add).then_inc(T.sem.near, 1)
+
+        p.wait_ge(T.sem.qsel, TILES)
+        p.wait_ge(T.sem.act, 2 * TILES)
+        p.wait_ge(T.sem.t0in, 2 * ne)
+        for i in range(TILES):
+            p.matmul_mx(bank(i), tile(T.selq, i), tile(T.sels, i), T.t0q[:], T.t0s[:], True, False)
+        p.wait_ge(T.sem.t1in, 2 * ne)
+        for i in range(TILES):
+            p.matmul_mx(bank(i), tile(T.selq, i), tile(T.sels, i), T.t1q[:], T.t1s[:], False, True).then_inc(T.sem.pu, 1)
+        v.wait_ge(T.sem.near, 1)
+        for i in range(TILES):
+            v.wait_ge(T.sem.pu, i + 1)
+            v.tensor_tensor(T.yo[:, i:W:4], bank(i), T.near[:, i:W:4], AluOpType.add).then_inc(T.sem.vy, 1)
+        g.sync.wait_ge(T.sem.vy, TILES)
+        g.sync.dma_start(T.y[:], T.yo[:]).then_inc(T.sem.sty, 16)
+        g.sync.wait_ge(T.sem.sty, 16)
+        g.wait_ge(T.sem.sent, sent[0])
+        return
+
+    other = helpers[s, 1 - k]
+    g.wait_ge(T.sem.m0c, ne)
+    send(other, _u8(T.m1q[:]), _u8(T.m0q[:]), T.sem.m1in, off)
+    g.wait_ge(T.sem.m0p, ne)
+    send(other, T.m1s[:], T.m0s[:], T.sem.m1in, off)
+
+    p = g.tensor
+    p.wait_ge(T.sem.m0c, ne)
+    p.wait_ge(T.sem.m0p, ne)
+    p.wait_ge(T.sem.win, 2 * ne)
+    for i in range(TILES):
+        p.matmul_mx(bank(i), tile(T.wq, i), tile(T.ws, i), T.m0q[:], T.m0s[:], True, True).then_inc(T.sem.pe, 1)
+    p.wait_ge(T.sem.m1in, 2 * ne)
+    for i in range(TILES):
+        p.matmul_mx(bank(4 + i), tile(T.wq, i), tile(T.ws, i), T.m1q[:], T.m1s[:], True, True).then_inc(T.sem.pe, 1)
+    for c in range(2):
+        h = T["h%d" % c]
+        for i in range(TILES):
+            j = TILES * c + i
+            if i % 2 == 0:
+                g.scalar.wait_ge(T.sem.pe, j + 1)
+                g.scalar.activation(h[:, i:W:4], bank(j), RELU).then_inc(T.sem.act, 1)
+            else:
+                g.vector.wait_ge(T.sem.pe, j + 1)
+                g.vector.tensor_scalar(h[:, i:W:4], bank(j), 0.0, None, AluOpType.max).then_inc(T.sem.vec, 1)
+        g.vector.wait_ge(T.sem.act, 2 * (c + 1))
+        g.vector.wait_ge(T.sem.vec, 2 * (c + 1))
+        g.vector.quantize_mx(T["h%dq" % c][:], T["h%ds" % c][:], h[:]).then_inc(T.sem.qh, 1)
+        owner = ranks[s, k if c == 0 else 1 - k]
+        g.wait_ge(T.sem.qh, c + 1)
+        send(owner, _u8(T["t%dq" % c][:]), _u8(T["h%dq" % c][:]), T.sem["t%din" % c], off)
+        send(owner, T["t%ds" % c][:], T["h%ds" % c][:], T.sem["t%din" % c], off)
+    g.wait_ge(T.sem.sent, sent[0])

@@ -1,9 +1,11 @@
+from concourse.bass import DstId, RemoteDMATransfer
 from concourse.mybir import dt, AluOpType, ActivationFunctionType
 
 CODES = "float8_e4m3fn_x4"
 W = 512
 NC = 128
 TILES = 4
+HALF = NC // 2
 SIM_CORES = 512
 
 SCRATCH = {
@@ -15,22 +17,21 @@ SCRATCH = {
     "asc": ("sbuf", [128, TILES * NC], "uint8"),
     "noq": ("sbuf", [128, TILES * NC], CODES),
     "nos": ("sbuf", [128, TILES * NC], "uint8"),
-    "wq": ("sbuf", [128, TILES * NC], CODES),
-    "ws": ("sbuf", [128, TILES * NC], "uint8"),
+    "w0q": ("sbuf", [128, 2 * NC], CODES),
+    "w0s": ("sbuf", [128, 2 * NC], "uint8"),
+    "w1q": ("sbuf", [128, 2 * NC], CODES),
+    "w1s": ("sbuf", [128, 2 * NC], "uint8"),
     "m0q": ("sbuf", [128, NC], CODES),
     "m0s": ("sbuf", [128, NC], "uint8"),
     "m1q": ("sbuf", [128, NC], CODES),
     "m1s": ("sbuf", [128, NC], "uint8"),
-    "h0": ("sbuf", [128, W], "bfloat16"),
-    "h1": ("sbuf", [128, W], "bfloat16"),
-    "h0q": ("sbuf", [128, NC], CODES),
-    "h0s": ("sbuf", [128, NC], "uint8"),
-    "h1q": ("sbuf", [128, NC], CODES),
-    "h1s": ("sbuf", [128, NC], "uint8"),
-    "t0q": ("sbuf", [128, NC], CODES),
-    "t0s": ("sbuf", [128, NC], "uint8"),
-    "t1q": ("sbuf", [128, NC], CODES),
-    "t1s": ("sbuf", [128, NC], "uint8"),
+    "c0": ("sbuf", [128, W], "float32"),
+    "c1": ("sbuf", [128, W], "float32"),
+    "h": ("sbuf", [128, W], "bfloat16"),
+    "hq": ("sbuf", [128, NC], CODES),
+    "hs": ("sbuf", [128, NC], "uint8"),
+    "tq": ("sbuf", [128, NC], CODES),
+    "ts": ("sbuf", [128, NC], "uint8"),
     "ones": ("sbuf", [128, W], "bfloat16"),
     "sel": ("sbuf", [128, TILES * W], "bfloat16"),
     "selq": ("sbuf", [128, TILES * NC], CODES),
@@ -42,7 +43,7 @@ SCRATCH = {
     "ps": ("psum", [128, 512 * 8], "float32"),
 }
 SEMAPHORES = ["lb", "la0", "la1", "ones", "qb", "qa", "sel", "qsel", "pe", "pu", "act", "vec", "near", "vy", "sty",
-              "nin", "win", "m0c", "m0p", "m1in", "qh", "t0in", "t1in", "sent"]
+              "nin", "w0in", "w1in", "m0c", "m0p", "m1in", "qh", "tin", "sent"]
 
 RELU = ActivationFunctionType.Relu
 _PLAN = {}
@@ -82,6 +83,11 @@ def _engines(mask):
     return bin(mask).count("1")
 
 
+def _halves(mask):
+    es = [e for e in range(16) if mask >> e & 1]
+    return [sum(1 << e for e in part) for part in (es[:len(es) // 2], es[len(es) // 2:])]
+
+
 def rank_program(g, core, T, topo):
     plan = _plan(T, topo)
     role = plan["role"].get(core)
@@ -100,6 +106,9 @@ def rank_program(g, core, T, topo):
     def tile(buf, i):
         return buf[:, NC * i:NC * i + NC]
 
+    def pair(buf, h):
+        return buf[:, 2 * NC * h:2 * NC * (h + 1)]
+
     kind, s, k = role
     ranks, helpers = plan["rank"], plan["helper"]
     off = topo.mask(ranks[s, k], helpers[s, k])
@@ -107,39 +116,41 @@ def rank_program(g, core, T, topo):
 
     if kind == "rank":
         mate = ranks[s, 1 - k]
-        mine = helpers[s, k]
-        far = helpers[1 - s, k]
         onchip = topo.mask(core, mate) & ~off
         nn = _engines(onchip)
+        order = (k, 1 - k)
 
         g.sync.dma_start(T.bbf[:], T.b[:]).then_inc(T.sem.lb, 16)
-        g.scalar.dma_start(T.abf[:, 0:2 * W], T.a[:, 0:2 * W]).then_inc(T.sem.la0, 16)
-        g.sync.dma_start(T.abf[:, 2 * W:4 * W], T.a[:, 2 * W:4 * W]).then_inc(T.sem.la1, 16)
+        for n, h in enumerate(order):
+            q = g.scalar if n == 0 else g.sync
+            q.dma_start(T.abf[:, 2 * W * h:2 * W * (h + 1)],
+                        T.a[:, 2 * W * h:2 * W * (h + 1)]).then_inc(T.sem["la%d" % n], 16)
 
         v = g.vector
         v.memset(T.ones[:], 1.0).then_inc(T.sem.ones, 1)
         v.wait_ge(T.sem.lb, 16)
         v.quantize_mx(T.bq[:], T.bs[:], T.bbf[:]).then_inc(T.sem.qb, 1)
-        for h in range(2):
-            v.wait_ge(T.sem["la%d" % h], 16)
-            v.quantize_mx(T.aq[:, 2 * NC * h:2 * NC * (h + 1)], T.asc[:, 2 * NC * h:2 * NC * (h + 1)],
-                          T.abf[:, 2 * W * h:2 * W * (h + 1)]).then_inc(T.sem.qa, 1)
+        for n, h in enumerate(order):
+            v.wait_ge(T.sem["la%d" % n], 16)
+            v.quantize_mx(pair(T.aq, h), pair(T.asc, h), T.abf[:, 2 * W * h:2 * W * (h + 1)]).then_inc(T.sem.qa, 1)
 
         g.wait_ge(T.sem.qb, 1)
-        send(mine, _u8(T.m0q[:]), _u8(T.bq[:]), T.sem.m0c, off)
-        send(mine, T.m0s[:], T.bs[:], T.sem.m0p, off)
-        g.wait_ge(T.sem.qa, 2)
-        send(far, _u8(T.wq[:]), _u8(T.aq[:]), T.sem.win, off)
-        send(far, T.ws[:], T.asc[:], T.sem.win, off)
+        send(helpers[s, k], _u8(T.m0q[:]), _u8(T.bq[:]), T.sem.m0c, off)
+        send(helpers[s, k], T.m0s[:], T.bs[:], T.sem.m0p, off)
+        for n, h in enumerate(order):
+            g.wait_ge(T.sem.qa, n + 1)
+            sem = T.sem["w%din" % n]
+            send(helpers[1 - s, h], _u8(T["w%dq" % n][:]), _u8(pair(T.aq, h)), sem, off)
+            send(helpers[1 - s, h], T["w%ds" % n][:], pair(T.asc, h), sem, off)
         send(mate, _u8(T.noq[:]), _u8(T.aq[:]), T.sem.nin, onchip)
         send(mate, T.nos[:], T.asc[:], T.sem.nin, onchip)
         g.wait_ge(T.sem.ones, 1)
-        for i in range(TILES):
-            g.affine_select(T.sel[:, W * i:W * i + W], T.ones[:], [[1, W]], AluOpType.is_equal, 0.0, -i,
+        for t in range(4):
+            g.affine_select(T.sel[:, W * t:W * t + W], T.ones[:], [[1, W]], AluOpType.is_equal, 0.0, -t,
                             -4).then_inc(T.sem.sel, 1)
-        for i in range(TILES):
-            v.wait_ge(T.sem.sel, i + 1)
-            v.quantize_mx(tile(T.selq, i), tile(T.sels, i), T.sel[:, W * i:W * i + W]).then_inc(T.sem.qsel, 1)
+        for t in range(4):
+            v.wait_ge(T.sem.sel, t + 1)
+            v.quantize_mx(tile(T.selq, t), tile(T.sels, t), T.sel[:, W * t:W * t + W]).then_inc(T.sem.qsel, 1)
 
         p = g.tensor
         p.wait_ge(T.sem.qb, 1)
@@ -157,19 +168,19 @@ def rank_program(g, core, T, topo):
         v.wait_ge(T.sem.act, 2 * TILES)
         v.tensor_tensor(T.near[:], T.own[:], T.nei[:], AluOpType.add).then_inc(T.sem.near, 1)
 
-        p.wait_ge(T.sem.qsel, TILES)
+        p.wait_ge(T.sem.qsel, 4)
         p.wait_ge(T.sem.act, 2 * TILES)
-        p.wait_ge(T.sem.t0in, 2 * ne)
-        for i in range(TILES):
-            p.matmul_mx(bank(i), tile(T.selq, i), tile(T.sels, i), T.t0q[:], T.t0s[:], True, False)
-        p.wait_ge(T.sem.t1in, 2 * ne)
-        for i in range(TILES):
-            p.matmul_mx(bank(i), tile(T.selq, i), tile(T.sels, i), T.t1q[:], T.t1s[:], False, True).then_inc(T.sem.pu, 1)
+        p.wait_ge(T.sem.tin, 2 * ne)
+        for t in range(4):
+            p.matmul_mx(bank(t), tile(T.selq, t), tile(T.sels, t), T.tq[:], T.ts[:], True, True).then_inc(T.sem.pu, 1)
         v.wait_ge(T.sem.near, 1)
-        for i in range(TILES):
-            v.wait_ge(T.sem.pu, i + 1)
-            v.tensor_tensor(T.yo[:, i:W:4], bank(i), T.near[:, i:W:4], AluOpType.add).then_inc(T.sem.vy, 1)
-        g.sync.wait_ge(T.sem.vy, TILES)
+        for t in range(4):
+            v.wait_ge(T.sem.pu, t + 1)
+            for h in range(2):
+                y0 = 4 * (t // 2) + 2 * h + t % 2
+                v.tensor_tensor(T.yo[:, y0:W:8], T.ps[:, 512 * t + HALF * h:512 * t + HALF * (h + 1)],
+                                T.near[:, y0:W:8], AluOpType.add).then_inc(T.sem.vy, 1)
+        g.sync.wait_ge(T.sem.vy, 8)
         g.sync.dma_start(T.y[:], T.yo[:]).then_inc(T.sem.sty, 16)
         g.sync.wait_ge(T.sem.sty, 16)
         g.wait_ge(T.sem.sent, sent[0])
@@ -181,30 +192,41 @@ def rank_program(g, core, T, topo):
     g.wait_ge(T.sem.m0p, ne)
     send(other, T.m1s[:], T.m0s[:], T.sem.m1in, off)
 
-    p = g.tensor
+    p, v = g.tensor, g.vector
     p.wait_ge(T.sem.m0c, ne)
     p.wait_ge(T.sem.m0p, ne)
-    p.wait_ge(T.sem.win, 2 * ne)
-    for i in range(TILES):
-        p.matmul_mx(bank(i), tile(T.wq, i), tile(T.ws, i), T.m0q[:], T.m0s[:], True, True).then_inc(T.sem.pe, 1)
-    p.wait_ge(T.sem.m1in, 2 * ne)
-    for i in range(TILES):
-        p.matmul_mx(bank(4 + i), tile(T.wq, i), tile(T.ws, i), T.m1q[:], T.m1s[:], True, True).then_inc(T.sem.pe, 1)
-    for c in range(2):
-        h = T["h%d" % c]
-        for i in range(TILES):
-            j = TILES * c + i
-            if i % 2 == 0:
+    for n in range(2):
+        p.wait_ge(T.sem["w%din" % n], 2 * ne)
+        for d in range(2):
+            if n == 0 and d == 1:
+                p.wait_ge(T.sem.m1in, 2 * ne)
+            for i in range(2):
+                p.matmul_mx(bank(4 * n + 2 * d + i), tile(T["w%dq" % n], i), tile(T["w%ds" % n], i),
+                            T["m%dq" % d][:], T["m%ds" % d][:], True, True).then_inc(T.sem.pe, 1)
+    for n in range(2):
+        for d in range(2):
+            at = 2 * HALF * 2 * (k if d == 0 else 1 - k)
+            for i in range(2):
+                j = 4 * n + 2 * d + i
                 g.scalar.wait_ge(T.sem.pe, j + 1)
-                g.scalar.activation(h[:, i:W:4], bank(j), RELU).then_inc(T.sem.act, 1)
-            else:
-                g.vector.wait_ge(T.sem.pe, j + 1)
-                g.vector.tensor_scalar(h[:, i:W:4], bank(j), 0.0, None, AluOpType.max).then_inc(T.sem.vec, 1)
-        g.vector.wait_ge(T.sem.act, 2 * (c + 1))
-        g.vector.wait_ge(T.sem.vec, 2 * (c + 1))
-        g.vector.quantize_mx(T["h%dq" % c][:], T["h%ds" % c][:], h[:]).then_inc(T.sem.qh, 1)
-        owner = ranks[s, k if c == 0 else 1 - k]
-        g.wait_ge(T.sem.qh, c + 1)
-        send(owner, _u8(T["t%dq" % c][:]), _u8(T["h%dq" % c][:]), T.sem["t%din" % c], off)
-        send(owner, T["t%ds" % c][:], T["h%ds" % c][:], T.sem["t%din" % c], off)
+                g.scalar.activation(T["c%d" % n][:, at + i:at + W // 2:2], bank(j), RELU).then_inc(T.sem.act, 1)
+                if n == 1:
+                    v.wait_ge(T.sem.act, j + 1)
+                    v.tensor_tensor(T.h[:, at + i:at + W // 2:2], T.c0[:, at + i:at + W // 2:2],
+                                    T.c1[:, at + i:at + W // 2:2], AluOpType.add).then_inc(T.sem.vec, 1)
+    v.wait_ge(T.sem.vec, 4)
+    v.quantize_mx(T.hq[:], T.hs[:], T.h[:]).then_inc(T.sem.qh, 1)
+
+    g.wait_ge(T.sem.qh, 1)
+    land = slice(HALF * k, HALF * (k + 1))
+    for codes in (True, False):
+        moves = []
+        for c, mask in enumerate(_halves(off)):
+            rid, pid = topo.addr(ranks[s, c], core)
+            words = slice(HALF * c, HALF * (c + 1))
+            src, dst = (_u8(T.hq[:, words]), _u8(T.tq[:, land])) if codes else (T.hs[:, words], T.ts[:, land])
+            moves.append(RemoteDMATransfer(dst_ids=[DstId(rid=rid, pnc=pid)], dma_engine_mask=mask,
+                                           remote_sem=T.sem.tin, src=src, dst=dst))
+        g.remote_dma_fused(moves, local_sem=T.sem.sent)
+        sent[0] += ne
     g.wait_ge(T.sem.sent, sent[0])

@@ -7,6 +7,9 @@ NC = 128
 TILES = 4
 HALF = NC // 2
 SIM_CORES = 512
+HOSTS = 4
+PLANE = 2
+RELAYS = (0, 1, PLANE)
 
 SCRATCH = {
     "bbf": ("sbuf", [128, W], "bfloat16"),
@@ -17,23 +20,22 @@ SCRATCH = {
     "asc": ("sbuf", [128, TILES * NC], "uint8"),
     "noq": ("sbuf", [128, TILES * NC], CODES),
     "nos": ("sbuf", [128, TILES * NC], "uint8"),
-    "w0q": ("sbuf", [128, 2 * NC], CODES),
-    "w0s": ("sbuf", [128, 2 * NC], "uint8"),
-    "w1q": ("sbuf", [128, 2 * NC], CODES),
-    "w1s": ("sbuf", [128, 2 * NC], "uint8"),
-    "m0q": ("sbuf", [128, NC], CODES),
-    "m0s": ("sbuf", [128, NC], "uint8"),
-    "m1q": ("sbuf", [128, NC], CODES),
-    "m1s": ("sbuf", [128, NC], "uint8"),
-    "c0": ("sbuf", [128, W], "float32"),
-    "c1": ("sbuf", [128, W], "float32"),
-    "h": ("sbuf", [128, W], "bfloat16"),
-    "hq": ("sbuf", [128, NC], CODES),
-    "hs": ("sbuf", [128, NC], "uint8"),
+    "fbq": ("sbuf", [128, NC], CODES),
+    "fbs": ("sbuf", [128, NC], "uint8"),
+    "fo": ("sbuf", [128, W], "float32"),
+    "fn": ("sbuf", [128, W], "float32"),
+    "h0": ("sbuf", [128, W], "bfloat16"),
+    "h1": ("sbuf", [128, W], "bfloat16"),
+    "hq": ("sbuf", [128, NC + HALF], CODES),
+    "hs": ("sbuf", [128, NC + HALF], "uint8"),
     "tq": ("sbuf", [128, NC], CODES),
     "ts": ("sbuf", [128, NC], "uint8"),
+    "rbq": ("sbuf", [128, HALF], CODES),
+    "rbs": ("sbuf", [128, NC], "uint8"),
+    "rtq": ("sbuf", [128, HALF], CODES),
+    "rts": ("sbuf", [128, NC], "uint8"),
     "ones": ("sbuf", [128, W], "bfloat16"),
-    "sel": ("sbuf", [128, TILES * W], "bfloat16"),
+    "sel": ("sbuf", [128, W], "bfloat16"),
     "selq": ("sbuf", [128, TILES * NC], CODES),
     "sels": ("sbuf", [128, TILES * NC], "uint8"),
     "own": ("sbuf", [128, W], "float32"),
@@ -42,8 +44,8 @@ SCRATCH = {
     "yo": ("sbuf", [128, W], "float32"),
     "ps": ("psum", [128, 512 * 8], "float32"),
 }
-SEMAPHORES = ["lb", "la0", "la1", "ones", "qb", "qa", "sel", "qsel", "pe", "pu", "act", "vec", "near", "vy", "sty",
-              "nin", "w0in", "w1in", "m0c", "m0p", "m1in", "qh", "tin", "sent"]
+SEMAPHORES = ["lb", "la0", "la1", "ones", "hz", "qb", "qa", "sel", "qsel", "selin", "pe", "pu", "act", "max", "vec",
+              "near", "vy", "sty", "nin0", "nin1", "fbin", "tin", "rbin", "rtin", "qh", "sent"]
 
 RELU = ActivationFunctionType.Relu
 _PLAN = {}
@@ -56,22 +58,25 @@ def _plan(T, topo):
     for c in T.cores:
         if topo.host(c) not in sides:
             sides.append(topo.host(c))
-
-    def place(c):
-        return sum(1 for d in range(c) if topo.host(d) == topo.host(c) and topo.chip(d) == topo.chip(c))
-
-    ranks, helpers = {}, {}
+    ranks, relays = {}, {}
     for s, h in enumerate(sides):
+        mid = [x for x in range(HOSTS) if x not in sides and topo.rack(x) == topo.rack(sides[1 - s])][0]
         for k, c in enumerate([c for c in T.cores if topo.host(c) == h]):
             ranks[s, k] = c
-            other = sides[1 - s]
-            for d in range(SIM_CORES):
-                if (topo.host(d) not in sides and topo.chip(d) == topo.chip(c)
-                        and topo.rack(topo.host(d)) == topo.rack(other) and place(d) == place(c)):
-                    helpers[s, k] = d
-    _PLAN.update({"rank": ranks, "helper": helpers,
+
+            def die(host):
+                return [d for d in range(SIM_CORES)
+                        if topo.host(d) == host and topo.chip(d) == topo.chip(c) and topo.die(d) == topo.die(c)]
+            home = die(h).index(c)
+            there = die(mid)
+            places = range(len(there))
+            apart = max(places, key=lambda n: abs(n - home))
+            beside = min([n for n in places if n != apart], key=lambda n: abs(n - apart))
+            for part, n in ((0, beside), (1, home), (PLANE, apart)):
+                relays[s, k, part] = there[n]
+    _PLAN.update({"rank": ranks, "relay": relays,
                   "role": dict([(c, ("rank",) + sk) for sk, c in ranks.items()]
-                               + [(c, ("helper",) + sk) for sk, c in helpers.items()])})
+                               + [(c, ("relay",) + skp) for skp, c in relays.items()])})
     return _PLAN
 
 
@@ -84,8 +89,31 @@ def _engines(mask):
 
 
 def _halves(mask):
-    es = [e for e in range(16) if mask >> e & 1]
+    es = [e for e in range(mask.bit_length()) if mask >> e & 1]
     return [sum(1 << e for e in part) for part in (es[:len(es) // 2], es[len(es) // 2:])]
+
+
+def _tile(buf, i):
+    return buf[:, NC * i:NC * i + NC]
+
+
+def _pair(buf, n, w=NC):
+    return buf[:, 2 * w * n:2 * w * (n + 1)]
+
+
+def _words(n):
+    return slice(HALF * n, HALF * (n + 1))
+
+
+def _bank(T, n):
+    return T.ps[:, 512 * n:512 * n + NC]
+
+
+def _selection(g, T, t):
+    g.wait_ge(T.sem.ones, 1)
+    g.affine_select(T.sel[:], T.ones[:], [[1, W]], AluOpType.is_equal, 0.0, -t, -4).then_inc(T.sem.sel, 1)
+    g.vector.wait_ge(T.sem.sel, 1)
+    g.vector.quantize_mx(_tile(T.selq, t), _tile(T.sels, t), T.sel[:]).then_inc(T.sem.qsel, 1)
 
 
 def rank_program(g, core, T, topo):
@@ -93,140 +121,138 @@ def rank_program(g, core, T, topo):
     role = plan["role"].get(core)
     if role is None:
         return
+    ranks, relays = plan["rank"], plan["relay"]
+    kind, s, k = role[:3]
     sent = [0]
 
-    def send(dst, out, in_, sem, mask):
-        rid, pid = topo.addr(dst, core)
-        g.remote_dma(out, in_, sem, T.sem.sent, pid, rid, mask)
+    def send(sem, mask, *pieces):
+        moves = []
+        for (dst, out, in_), part in zip(pieces, [mask] if len(pieces) == 1 else _halves(mask)):
+            rid, pid = topo.addr(dst, core)
+            moves.append(RemoteDMATransfer(dst_ids=[DstId(rid=rid, pnc=pid)], dma_engine_mask=part, remote_sem=sem,
+                                           src=in_, dst=out))
+        g.remote_dma_fused(moves, local_sem=T.sem.sent)
         sent[0] += _engines(mask)
 
-    def bank(k):
-        return T.ps[:, 512 * k:512 * k + NC]
-
-    def tile(buf, i):
-        return buf[:, NC * i:NC * i + NC]
-
-    def pair(buf, h):
-        return buf[:, 2 * NC * h:2 * NC * (h + 1)]
-
-    kind, s, k = role
-    ranks, helpers = plan["rank"], plan["helper"]
-    off = topo.mask(ranks[s, k], helpers[s, k])
-    ne = _engines(off)
-
-    if kind == "rank":
-        mate = ranks[s, 1 - k]
-        onchip = topo.mask(core, mate) & ~off
-        nn = _engines(onchip)
-        order = (k, 1 - k)
-
-        g.sync.dma_start(T.bbf[:], T.b[:]).then_inc(T.sem.lb, 16)
-        for n, h in enumerate(order):
-            q = g.scalar if n == 0 else g.sync
-            q.dma_start(T.abf[:, 2 * W * h:2 * W * (h + 1)],
-                        T.a[:, 2 * W * h:2 * W * (h + 1)]).then_inc(T.sem["la%d" % n], 16)
-
-        v = g.vector
-        v.memset(T.ones[:], 1.0).then_inc(T.sem.ones, 1)
-        v.wait_ge(T.sem.lb, 16)
-        v.quantize_mx(T.bq[:], T.bs[:], T.bbf[:]).then_inc(T.sem.qb, 1)
-        for n, h in enumerate(order):
-            v.wait_ge(T.sem["la%d" % n], 16)
-            v.quantize_mx(pair(T.aq, h), pair(T.asc, h), T.abf[:, 2 * W * h:2 * W * (h + 1)]).then_inc(T.sem.qa, 1)
-
-        g.wait_ge(T.sem.qb, 1)
-        send(helpers[s, k], _u8(T.m0q[:]), _u8(T.bq[:]), T.sem.m0c, off)
-        send(helpers[s, k], T.m0s[:], T.bs[:], T.sem.m0p, off)
-        for n, h in enumerate(order):
-            g.wait_ge(T.sem.qa, n + 1)
-            sem = T.sem["w%din" % n]
-            send(helpers[1 - s, h], _u8(T["w%dq" % n][:]), _u8(pair(T.aq, h)), sem, off)
-            send(helpers[1 - s, h], T["w%ds" % n][:], pair(T.asc, h), sem, off)
-        send(mate, _u8(T.noq[:]), _u8(T.aq[:]), T.sem.nin, onchip)
-        send(mate, T.nos[:], T.asc[:], T.sem.nin, onchip)
-        g.wait_ge(T.sem.ones, 1)
-        for t in range(4):
-            g.affine_select(T.sel[:, W * t:W * t + W], T.ones[:], [[1, W]], AluOpType.is_equal, 0.0, -t,
-                            -4).then_inc(T.sem.sel, 1)
-        for t in range(4):
-            v.wait_ge(T.sem.sel, t + 1)
-            v.quantize_mx(tile(T.selq, t), tile(T.sels, t), T.sel[:, W * t:W * t + W]).then_inc(T.sem.qsel, 1)
-
-        p = g.tensor
-        p.wait_ge(T.sem.qb, 1)
-        p.wait_ge(T.sem.qa, 2)
-        for i in range(TILES):
-            p.matmul_mx(bank(i), tile(T.aq, i), tile(T.asc, i), T.bq[:], T.bs[:], True, True).then_inc(T.sem.pe, 1)
-        p.wait_ge(T.sem.nin, 2 * nn)
-        for i in range(TILES):
-            p.matmul_mx(bank(4 + i), tile(T.noq, i), tile(T.nos, i), T.bq[:], T.bs[:], True, True).then_inc(T.sem.pe, 1)
-        for j in range(2 * TILES):
-            g.scalar.wait_ge(T.sem.pe, j + 1)
-            dst = T.own if j < TILES else T.nei
-            i = j % TILES
-            g.scalar.activation(dst[:, i:W:4], bank(j), RELU).then_inc(T.sem.act, 1)
-        v.wait_ge(T.sem.act, 2 * TILES)
-        v.tensor_tensor(T.near[:], T.own[:], T.nei[:], AluOpType.add).then_inc(T.sem.near, 1)
-
-        p.wait_ge(T.sem.qsel, 4)
-        p.wait_ge(T.sem.act, 2 * TILES)
-        p.wait_ge(T.sem.tin, 2 * ne)
-        for t in range(4):
-            p.matmul_mx(bank(t), tile(T.selq, t), tile(T.sels, t), T.tq[:], T.ts[:], True, True).then_inc(T.sem.pu, 1)
-        v.wait_ge(T.sem.near, 1)
-        for t in range(4):
-            v.wait_ge(T.sem.pu, t + 1)
-            for h in range(2):
-                y0 = 4 * (t // 2) + 2 * h + t % 2
-                v.tensor_tensor(T.yo[:, y0:W:8], T.ps[:, 512 * t + HALF * h:512 * t + HALF * (h + 1)],
-                                T.near[:, y0:W:8], AluOpType.add).then_inc(T.sem.vy, 1)
-        g.sync.wait_ge(T.sem.vy, 8)
-        g.sync.dma_start(T.y[:], T.yo[:]).then_inc(T.sem.sty, 16)
-        g.sync.wait_ge(T.sem.sty, 16)
-        g.wait_ge(T.sem.sent, sent[0])
-        return
-
-    other = helpers[s, 1 - k]
-    g.wait_ge(T.sem.m0c, ne)
-    send(other, _u8(T.m1q[:]), _u8(T.m0q[:]), T.sem.m1in, off)
-    g.wait_ge(T.sem.m0p, ne)
-    send(other, T.m1s[:], T.m0s[:], T.sem.m1in, off)
-
-    p, v = g.tensor, g.vector
-    p.wait_ge(T.sem.m0c, ne)
-    p.wait_ge(T.sem.m0p, ne)
-    for n in range(2):
-        p.wait_ge(T.sem["w%din" % n], 2 * ne)
-        for d in range(2):
-            if n == 0 and d == 1:
-                p.wait_ge(T.sem.m1in, 2 * ne)
-            for i in range(2):
-                p.matmul_mx(bank(4 * n + 2 * d + i), tile(T["w%dq" % n], i), tile(T["w%ds" % n], i),
-                            T["m%dq" % d][:], T["m%ds" % d][:], True, True).then_inc(T.sem.pe, 1)
-    for n in range(2):
-        for d in range(2):
-            at = 2 * HALF * 2 * (k if d == 0 else 1 - k)
-            for i in range(2):
-                j = 4 * n + 2 * d + i
-                g.scalar.wait_ge(T.sem.pe, j + 1)
-                g.scalar.activation(T["c%d" % n][:, at + i:at + W // 2:2], bank(j), RELU).then_inc(T.sem.act, 1)
-                if n == 1:
-                    v.wait_ge(T.sem.act, j + 1)
-                    v.tensor_tensor(T.h[:, at + i:at + W // 2:2], T.c0[:, at + i:at + W // 2:2],
-                                    T.c1[:, at + i:at + W // 2:2], AluOpType.add).then_inc(T.sem.vec, 1)
-    v.wait_ge(T.sem.vec, 4)
-    v.quantize_mx(T.hq[:], T.hs[:], T.h[:]).then_inc(T.sem.qh, 1)
-
-    g.wait_ge(T.sem.qh, 1)
-    land = slice(HALF * k, HALF * (k + 1))
-    for codes in (True, False):
-        moves = []
-        for c, mask in enumerate(_halves(off)):
-            rid, pid = topo.addr(ranks[s, c], core)
-            words = slice(HALF * c, HALF * (c + 1))
-            src, dst = (_u8(T.hq[:, words]), _u8(T.tq[:, land])) if codes else (T.hs[:, words], T.ts[:, land])
-            moves.append(RemoteDMATransfer(dst_ids=[DstId(rid=rid, pnc=pid)], dma_engine_mask=mask,
-                                           remote_sem=T.sem.tin, src=src, dst=dst))
-        g.remote_dma_fused(moves, local_sem=T.sem.sent)
-        sent[0] += ne
+    if kind == "relay":
+        _relay(g, core, T, topo, send, ranks[s, k], ranks[1 - s, k], role[3])
+    else:
+        _rank(g, core, T, topo, send, ranks[s, 1 - k], [relays[1 - s, k, part] for part in RELAYS])
     g.wait_ge(T.sem.sent, sent[0])
+
+
+def _relay(g, core, T, topo, send, near, far, part):
+    off, back = topo.mask(core, near), topo.mask(core, far)
+    ne = _engines(off)
+    g.vector.memset(T.ones[:], 1.0).then_inc(T.sem.ones, 1)
+    _selection(g, T, part)
+    g.wait_ge(T.sem.qsel, 1)
+    send(T.sem.selin, back, (far, _u8(_tile(T.selq, part)), _u8(_tile(T.selq, part))))
+    send(T.sem.selin, back, (far, _tile(T.sels, part), _tile(T.sels, part)))
+    if part == PLANE:
+        g.wait_ge(T.sem.rbin, ne)
+        send(T.sem.fbin, off, (near, T.fbs[:], T.rbs[:]))
+        g.wait_ge(T.sem.rtin, ne)
+        send(T.sem.tin, off, (near, T.ts[:], T.rts[:]))
+    else:
+        g.wait_ge(T.sem.rbin, ne // 2)
+        send(T.sem.fbin, off, (near, _u8(T.fbq[:, _words(part)]), _u8(T.rbq[:])))
+        g.wait_ge(T.sem.rtin, ne)
+        send(T.sem.tin, off, (near, _u8(T.tq[:, _words(part)]), _u8(T.rtq[:])))
+
+
+def _rank(g, core, T, topo, send, mate, hops):
+    off = topo.mask(core, hops[PLANE])
+    ne = _engines(off)
+    every = topo.mask(core, mate)
+    masks = (every & ~off, every)
+    v, p = g.vector, g.tensor
+
+    g.sync.dma_start(T.bbf[:], T.b[:]).then_inc(T.sem.lb, 16)
+    for n in range(2):
+        g.sync.dma_start(_pair(T.abf, n, W), _pair(T.a, n, W)).then_inc(T.sem["la%d" % n], 16)
+
+    v.memset(T.ones[:], 1.0).then_inc(T.sem.ones, 1)
+    for n in range(2):
+        v.memset(T["h%d" % n][:, W // 2:], 0.0).then_inc(T.sem.hz, 1)
+    v.wait_ge(T.sem.lb, 16)
+    v.quantize_mx(T.bq[:], T.bs[:], T.bbf[:]).then_inc(T.sem.qb, 1)
+    for n in range(2):
+        v.wait_ge(T.sem["la%d" % n], 16)
+        v.quantize_mx(_pair(T.aq, n), _pair(T.asc, n), _pair(T.abf, n, W)).then_inc(T.sem.qa, 1)
+
+    g.wait_ge(T.sem.qb, 1)
+    send(T.sem.rbin, off, *[(hops[n], _u8(T.rbq[:]), _u8(T.bq[:, _words(n)])) for n in range(2)])
+    send(T.sem.rbin, off, (hops[PLANE], T.rbs[:], T.bs[:]))
+    for n in range(2):
+        g.wait_ge(T.sem.qa, n + 1)
+        send(T.sem["nin%d" % n], masks[n], (mate, _u8(_pair(T.noq, n)), _u8(_pair(T.aq, n))))
+        send(T.sem["nin%d" % n], masks[n], (mate, _pair(T.nos, n), _pair(T.asc, n)))
+    _selection(g, T, TILES - 1)
+
+    own_b, far_b = (T.bq, T.bs), (T.fbq, T.fbs)
+    own_a, nei_a = (T.aq, T.asc), (T.noq, T.nos)
+    todo = [(own_a, i, own_b, i, T.own) for i in range(TILES)]
+    for n in range(2):
+        two = (2 * n, 2 * n + 1)
+        todo += [(own_a, i, far_b, 4 + i, T.fo) for i in two] + [(nei_a, i, far_b, i, T.fn) for i in two]
+    todo += [(nei_a, i, own_b, 4 + i, T.nei) for i in range(TILES)]
+    last = {}
+    acts = 0
+    p.wait_ge(T.sem.qb, 1)
+    p.wait_ge(T.sem.qa, 2)
+    for j, (a, i, b, at, dst) in enumerate(todo):
+        if j == TILES:
+            p.wait_ge(T.sem.fbin, 3 * ne)
+        if dst is T.fn and i % 2 == 0:
+            p.wait_ge(T.sem["nin%d" % (i // 2)], 2 * _engines(masks[i // 2]))
+        if at in last:
+            p.wait_ge(T.sem.act, last[at])
+        p.matmul_mx(_bank(T, at), _tile(a[0], i), _tile(a[1], i), b[0][:], b[1][:], True, True).then_inc(T.sem.pe, 1)
+        if dst is T.fn and i % 2 == 0:
+            v.wait_ge(T.sem.pe, j + 1)
+            v.tensor_scalar(T.fn[:, i:W:4], _bank(T, at), 0.0, None, AluOpType.max).then_inc(T.sem.max, 1)
+            two_own = acts
+        else:
+            g.scalar.wait_ge(T.sem.pe, j + 1)
+            g.scalar.activation(dst[:, i:W:4], _bank(T, at), RELU).then_inc(T.sem.act, 1)
+            acts += 1
+            last[at] = acts
+        if dst is T.fn and i % 2 == 1:
+            n = i // 2
+            if n == 0:
+                v.wait_ge(T.sem.hz, 2)
+            v.wait_ge(T.sem.max, n + 1)
+            for m, count in ((i - 1, two_own), (i, acts)):
+                v.wait_ge(T.sem.act, count)
+                v.tensor_tensor(T["h%d" % n][:, m % 2:W // 2:2], T.fo[:, m:W:4], T.fn[:, m:W:4],
+                                AluOpType.add).then_inc(T.sem.vec, 1)
+            v.wait_ge(T.sem.vec, 2 * (n + 1))
+            if n:
+                v.wait_ge(T.sem.qh, n)
+            words = slice(HALF * n, HALF * n + NC)
+            v.quantize_mx(T.hq[:, words], T.hs[:, words], T["h%d" % n][:]).then_inc(T.sem.qh, 1)
+            g.wait_ge(T.sem.qh, n + 1)
+            send(T.sem.rtin, off, (hops[n], _u8(T.rtq[:]), _u8(T.hq[:, _words(n)])))
+    send(T.sem.rtin, off, (hops[PLANE], T.rts[:], T.hs[:, :NC]))
+    v.wait_ge(T.sem.act, acts)
+    v.tensor_tensor(T.near[:], T.own[:], T.nei[:], AluOpType.add).then_inc(T.sem.near, 1)
+
+    p.wait_ge(T.sem.qsel, 1)
+    p.wait_ge(T.sem.selin, 2 * ne * len(RELAYS))
+    p.wait_ge(T.sem.act, acts)
+    p.wait_ge(T.sem.max, 2)
+    p.wait_ge(T.sem.tin, 3 * ne)
+    for t in range(TILES):
+        p.matmul_mx(_bank(T, t), _tile(T.selq, t), _tile(T.sels, t), T.tq[:], T.ts[:], True,
+                    True).then_inc(T.sem.pu, 1)
+    v.wait_ge(T.sem.near, 1)
+    for t in range(TILES):
+        v.wait_ge(T.sem.pu, t + 1)
+        for n in range(2):
+            y0 = 4 * (t // 2) + 2 * n + t % 2
+            v.tensor_tensor(T.yo[:, y0:W:8], T.ps[:, 512 * t + HALF * n:512 * t + HALF * (n + 1)], T.near[:, y0:W:8],
+                            AluOpType.add).then_inc(T.sem.vy, 1)
+    g.sync.wait_ge(T.sem.vy, 8)
+    g.sync.dma_start(T.y[:], T.yo[:]).then_inc(T.sem.sty, 16)
+    g.sync.wait_ge(T.sem.sty, 16)

@@ -34,20 +34,22 @@ SCRATCH = {
     "rbs": ("sbuf", [128, NC], "uint8"),
     "rtq": ("sbuf", [128, HALF], CODES),
     "rts": ("sbuf", [128, NC], "uint8"),
-    "ones": ("sbuf", [128, W], "bfloat16"),
     "sel": ("sbuf", [128, W], "bfloat16"),
     "selq": ("sbuf", [128, TILES * NC], CODES),
     "sels": ("sbuf", [128, TILES * NC], "uint8"),
     "own": ("sbuf", [128, W], "float32"),
     "nei": ("sbuf", [128, W], "float32"),
-    "near": ("sbuf", [128, W], "float32"),
+    "near": ("sbuf", [128, W], "bfloat16"),
+    "nq": ("sbuf", [128, NC], CODES),
+    "ns": ("sbuf", [128, NC], "uint8"),
     "yo": ("sbuf", [128, W], "float32"),
     "ps": ("psum", [128, 512 * 8], "float32"),
 }
-SEMAPHORES = ["lb", "la0", "la1", "ones", "hz", "qb", "qa", "sel", "qsel", "selin", "pe", "pu", "act", "max", "vec",
-              "near", "vy", "sty", "nin0", "nin1", "fbin", "tin", "rbin", "rtin", "qh", "sent"]
+SEMAPHORES = ["lb", "la0", "la1", "zero", "hz", "qb", "qa", "sel", "qsel", "selin", "pe", "pu", "act", "max", "vec",
+              "near", "qn", "vy0", "vy1", "sty", "nin", "fbin", "tin", "rbin", "rtin", "qh", "sent"]
 
 RELU = ActivationFunctionType.Relu
+COPY = ActivationFunctionType.Copy
 _PLAN = {}
 
 
@@ -59,8 +61,8 @@ def _plan(T, topo):
         if topo.host(c) not in sides:
             sides.append(topo.host(c))
     ranks, relays = {}, {}
+    mid = [[x for x in range(HOSTS) if x not in sides and topo.rack(x) == topo.rack(sides[1 - s])][0] for s in (0, 1)]
     for s, h in enumerate(sides):
-        mid = [x for x in range(HOSTS) if x not in sides and topo.rack(x) == topo.rack(sides[1 - s])][0]
         for k, c in enumerate([c for c in T.cores if topo.host(c) == h]):
             ranks[s, k] = c
 
@@ -68,12 +70,11 @@ def _plan(T, topo):
                 return [d for d in range(SIM_CORES)
                         if topo.host(d) == host and topo.chip(d) == topo.chip(c) and topo.die(d) == topo.die(c)]
             home = die(h).index(c)
-            there = die(mid)
-            places = range(len(there))
+            places = range(len(die(h)))
             apart = max(places, key=lambda n: abs(n - home))
             beside = min([n for n in places if n != apart], key=lambda n: abs(n - apart))
-            for part, n in ((0, beside), (1, home), (PLANE, apart)):
-                relays[s, k, part] = there[n]
+            relays[s, k, 0], relays[s, k, 1] = die(mid[s])[beside], die(mid[s])[home]
+            relays[s, k, PLANE] = die(mid[1 - s])[apart]
     _PLAN.update({"rank": ranks, "relay": relays,
                   "role": dict([(c, ("rank",) + sk) for sk, c in ranks.items()]
                                + [(c, ("relay",) + skp) for skp, c in relays.items()])})
@@ -109,11 +110,21 @@ def _bank(T, n):
     return T.ps[:, 512 * n:512 * n + NC]
 
 
-def _selection(g, T, t):
-    g.wait_ge(T.sem.ones, 1)
-    g.affine_select(T.sel[:], T.ones[:], [[1, W]], AluOpType.is_equal, 0.0, -t, -4).then_inc(T.sem.sel, 1)
+def _at(i):
+    return slice(W // 2 * (i // 2) + i % 2, W // 2 * (i // 2 + 1), 2)
+
+
+def _fill(g, T):
+    g.vector.memset(T.sel[:], 0.0).then_inc(T.sem.zero, 1)
+
+
+def _select(g, T, t):
+    g.wait_ge(T.sem.zero, 1)
+    view = T.sel[:, t:W:4]
+    g.affine_select(view, view, [[1, NC]], AluOpType.not_equal, 1.0, 0, -1).then_inc(T.sem.sel, 1)
     g.vector.wait_ge(T.sem.sel, 1)
     g.vector.quantize_mx(_tile(T.selq, t), _tile(T.sels, t), T.sel[:]).then_inc(T.sem.qsel, 1)
+    g.wait_ge(T.sem.qsel, 1)
 
 
 def rank_program(g, core, T, topo):
@@ -137,18 +148,20 @@ def rank_program(g, core, T, topo):
     if kind == "relay":
         _relay(g, core, T, topo, send, ranks[s, k], ranks[1 - s, k], role[3])
     else:
-        _rank(g, core, T, topo, send, ranks[s, 1 - k], [relays[1 - s, k, part] for part in RELAYS])
+        _rank(g, core, T, topo, send, k, ranks[s, 1 - k], [relays[1 - s, k, part] for part in RELAYS])
     g.wait_ge(T.sem.sent, sent[0])
 
 
 def _relay(g, core, T, topo, send, near, far, part):
-    off, back = topo.mask(core, near), topo.mask(core, far)
+    off = topo.mask(core, near)
     ne = _engines(off)
-    g.vector.memset(T.ones[:], 1.0).then_inc(T.sem.ones, 1)
-    _selection(g, T, part)
-    g.wait_ge(T.sem.qsel, 1)
-    send(T.sem.selin, back, (far, _u8(_tile(T.selq, part)), _u8(_tile(T.selq, part))))
-    send(T.sem.selin, back, (far, _tile(T.sels, part), _tile(T.sels, part)))
+    user = near if topo.same_plane(core, near) else far
+    t, first, last = (1, 0, NC) if part == PLANE else (0, HALF * part, HALF * (part + 1))
+    cols = slice(NC * t + first, NC * t + last)
+    _fill(g, T)
+    _select(g, T, t)
+    for view in (_u8(T.selq[:, cols]), T.sels[:, cols]):
+        send(T.sem.selin, topo.mask(core, user), (user, view, view))
     if part == PLANE:
         g.wait_ge(T.sem.rbin, ne)
         send(T.sem.fbin, off, (near, T.fbs[:], T.rbs[:]))
@@ -161,20 +174,25 @@ def _relay(g, core, T, topo, send, near, far, part):
         send(T.sem.tin, off, (near, _u8(T.tq[:, _words(part)]), _u8(T.rtq[:])))
 
 
-def _rank(g, core, T, topo, send, mate, hops):
+def _rank(g, core, T, topo, send, k, mate, hops):
     off = topo.mask(core, hops[PLANE])
     ne = _engines(off)
     every = topo.mask(core, mate)
     masks = (every & ~off, every)
+    mine = TILES - 2 + k
     v, p = g.vector, g.tensor
 
     g.sync.dma_start(T.bbf[:], T.b[:]).then_inc(T.sem.lb, 16)
-    for n in range(2):
-        g.sync.dma_start(_pair(T.abf, n, W), _pair(T.a, n, W)).then_inc(T.sem["la%d" % n], 16)
+    g.sync.dma_start(_pair(T.abf, 0, W), _pair(T.a, 0, W)).then_inc(T.sem.la0, 16)
+    g.sync.wait_ge(T.sem.qb, 1)
+    g.sync.dma_start(_pair(T.abf, 1, W), _pair(T.a, 1, W)).then_inc(T.sem.la1, 16)
 
-    v.memset(T.ones[:], 1.0).then_inc(T.sem.ones, 1)
+    _fill(g, T)
     for n in range(2):
         v.memset(T["h%d" % n][:, W // 2:], 0.0).then_inc(T.sem.hz, 1)
+    _select(g, T, mine)
+    send(T.sem.selin, off, (mate, _u8(_tile(T.selq, mine)), _u8(_tile(T.selq, mine))))
+
     v.wait_ge(T.sem.lb, 16)
     v.quantize_mx(T.bq[:], T.bs[:], T.bbf[:]).then_inc(T.sem.qb, 1)
     for n in range(2):
@@ -186,9 +204,9 @@ def _rank(g, core, T, topo, send, mate, hops):
     send(T.sem.rbin, off, (hops[PLANE], T.rbs[:], T.bs[:]))
     for n in range(2):
         g.wait_ge(T.sem.qa, n + 1)
-        send(T.sem["nin%d" % n], masks[n], (mate, _u8(_pair(T.noq, n)), _u8(_pair(T.aq, n))))
-        send(T.sem["nin%d" % n], masks[n], (mate, _pair(T.nos, n), _pair(T.asc, n)))
-    _selection(g, T, TILES - 1)
+        send(T.sem.nin, masks[n], (mate, _u8(_pair(T.noq, n)), _u8(_pair(T.aq, n))))
+    send(T.sem.nin, every, (mate, T.nos[:], T.asc[:]))
+    send(T.sem.selin, off, (mate, _tile(T.sels, mine), _tile(T.sels, mine)))
 
     own_b, far_b = (T.bq, T.bs), (T.fbq, T.fbs)
     own_a, nei_a = (T.aq, T.asc), (T.noq, T.nos)
@@ -199,33 +217,36 @@ def _rank(g, core, T, topo, send, mate, hops):
     todo += [(nei_a, i, own_b, 4 + i, T.nei) for i in range(TILES)]
     last = {}
     acts = 0
+    counts = {}
     p.wait_ge(T.sem.qb, 1)
     p.wait_ge(T.sem.qa, 2)
     for j, (a, i, b, at, dst) in enumerate(todo):
         if j == TILES:
             p.wait_ge(T.sem.fbin, 3 * ne)
-        if dst is T.fn and i % 2 == 0:
-            p.wait_ge(T.sem["nin%d" % (i // 2)], 2 * _engines(masks[i // 2]))
+        if dst is T.fn and i == 0:
+            p.wait_ge(T.sem.nin, _engines(masks[0]) + _engines(masks[1]) + _engines(every))
         if at in last:
             p.wait_ge(T.sem.act, last[at])
         p.matmul_mx(_bank(T, at), _tile(a[0], i), _tile(a[1], i), b[0][:], b[1][:], True, True).then_inc(T.sem.pe, 1)
-        if dst is T.fn and i % 2 == 0:
+        if dst is T.fn and i == 0:
             v.wait_ge(T.sem.pe, j + 1)
-            v.tensor_scalar(T.fn[:, i:W:4], _bank(T, at), 0.0, None, AluOpType.max).then_inc(T.sem.max, 1)
-            two_own = acts
+            v.tensor_scalar(T.fn[:, _at(i)], _bank(T, at), 0.0, None, AluOpType.max).then_inc(T.sem.max, 1)
+            counts[i] = acts
         else:
             g.scalar.wait_ge(T.sem.pe, j + 1)
-            g.scalar.activation(dst[:, i:W:4], _bank(T, at), RELU).then_inc(T.sem.act, 1)
+            g.scalar.activation(dst[:, _at(i)], _bank(T, at), RELU).then_inc(T.sem.act, 1)
             acts += 1
             last[at] = acts
+            if dst is T.fn:
+                counts[i] = acts
         if dst is T.fn and i % 2 == 1:
             n = i // 2
             if n == 0:
                 v.wait_ge(T.sem.hz, 2)
-            v.wait_ge(T.sem.max, n + 1)
-            for m, count in ((i - 1, two_own), (i, acts)):
-                v.wait_ge(T.sem.act, count)
-                v.tensor_tensor(T["h%d" % n][:, m % 2:W // 2:2], T.fo[:, m:W:4], T.fn[:, m:W:4],
+                v.wait_ge(T.sem.max, 1)
+            for m in (i - 1, i):
+                v.wait_ge(T.sem.act, counts[m])
+                v.tensor_tensor(T["h%d" % n][:, m % 2:W // 2:2], T.fo[:, _at(m)], T.fn[:, _at(m)],
                                 AluOpType.add).then_inc(T.sem.vec, 1)
             v.wait_ge(T.sem.vec, 2 * (n + 1))
             if n:
@@ -237,22 +258,31 @@ def _rank(g, core, T, topo, send, mate, hops):
     send(T.sem.rtin, off, (hops[PLANE], T.rts[:], T.hs[:, :NC]))
     v.wait_ge(T.sem.act, acts)
     v.tensor_tensor(T.near[:], T.own[:], T.nei[:], AluOpType.add).then_inc(T.sem.near, 1)
+    v.wait_ge(T.sem.near, 1)
+    v.quantize_mx(T.nq[:], T.ns[:], T.near[:]).then_inc(T.sem.qn, 1)
 
     p.wait_ge(T.sem.qsel, 1)
-    p.wait_ge(T.sem.selin, 2 * ne * len(RELAYS))
+    p.wait_ge(T.sem.selin, 8 * ne)
     p.wait_ge(T.sem.act, acts)
-    p.wait_ge(T.sem.max, 2)
+    p.wait_ge(T.sem.max, 1)
+    p.wait_ge(T.sem.qn, 1)
+    for t in range(TILES):
+        p.matmul_mx(_bank(T, t), _tile(T.selq, t), _tile(T.sels, t), T.nq[:], T.ns[:], True, False)
     p.wait_ge(T.sem.tin, 3 * ne)
     for t in range(TILES):
-        p.matmul_mx(_bank(T, t), _tile(T.selq, t), _tile(T.sels, t), T.tq[:], T.ts[:], True,
+        p.matmul_mx(_bank(T, t), _tile(T.selq, t), _tile(T.sels, t), T.tq[:], T.ts[:], False,
                     True).then_inc(T.sem.pu, 1)
-    v.wait_ge(T.sem.near, 1)
     for t in range(TILES):
-        v.wait_ge(T.sem.pu, t + 1)
-        for n in range(2):
-            y0 = 4 * (t // 2) + 2 * n + t % 2
-            v.tensor_tensor(T.yo[:, y0:W:8], T.ps[:, 512 * t + HALF * n:512 * t + HALF * (n + 1)], T.near[:, y0:W:8],
-                            AluOpType.add).then_inc(T.sem.vy, 1)
-    g.sync.wait_ge(T.sem.vy, 8)
-    g.sync.dma_start(T.y[:], T.yo[:]).then_inc(T.sem.sty, 16)
-    g.sync.wait_ge(T.sem.sty, 16)
+        q = g.scalar if t % 2 else v
+        q.wait_ge(T.sem.pu, t + 1)
+        for half in range(2):
+            for n in range(2):
+                y0 = W // 2 * half + 4 * (t // 2) + 2 * n + t % 2
+                x0 = 512 * t + HALF * n + HALF // 2 * half
+                to, of = T.yo[:, y0:W // 2 * (half + 1):8], T.ps[:, x0:x0 + HALF // 2]
+                (q.activation(to, of, COPY) if t % 2 else q.tensor_copy(to, of)).then_inc(T.sem["vy%d" % half], 1)
+    for half in range(2):
+        cols = slice(W // 2 * half, W // 2 * (half + 1))
+        g.sync.wait_ge(T.sem["vy%d" % half], 8)
+        g.sync.dma_start(T.y[:, cols], T.yo[:, cols]).then_inc(T.sem.sty, 16)
+    g.sync.wait_ge(T.sem.sty, 32)

from concourse.bass import DstId, RemoteDMATransfer
from concourse.mybir import dt, AluOpType, ActivationFunctionType

CODES = "float8_e4m3fn_x4"
W = 512
NC = 128
TILES = 4
HALF = NC // 2
SIM_CORES = 512
HOSTS = 4
PLANE = 2
RELAYS = (0, 1, PLANE)

SCRATCH = {
    "bbf": ("sbuf", [128, W], "bfloat16"),
    "abf": ("sbuf", [128, TILES * W], "bfloat16"),
    "bq": ("sbuf", [128, NC], CODES),
    "bs": ("sbuf", [128, NC], "uint8"),
    "aq": ("sbuf", [128, TILES * NC], CODES),
    "asc": ("sbuf", [128, TILES * NC], "uint8"),
    "noq": ("sbuf", [128, TILES * NC], CODES),
    "nos": ("sbuf", [128, TILES * NC], "uint8"),
    "fbq": ("sbuf", [128, NC], CODES),
    "fbs": ("sbuf", [128, NC], "uint8"),
    "fo": ("sbuf", [128, W], "float32"),
    "fn": ("sbuf", [128, W], "float32"),
    "h0": ("sbuf", [128, W], "bfloat16"),
    "h1": ("sbuf", [128, W], "bfloat16"),
    "hq": ("sbuf", [128, NC + HALF], CODES),
    "hs": ("sbuf", [128, NC + HALF], "uint8"),
    "tq": ("sbuf", [128, NC], CODES),
    "ts": ("sbuf", [128, NC], "uint8"),
    "rbq": ("sbuf", [128, HALF], CODES),
    "rbs": ("sbuf", [128, NC], "uint8"),
    "rtq": ("sbuf", [128, HALF], CODES),
    "rts": ("sbuf", [128, NC], "uint8"),
    "sel": ("sbuf", [128, W], "bfloat16"),
    "selq": ("sbuf", [128, TILES * NC], CODES),
    "sels": ("sbuf", [128, TILES * NC], "uint8"),
    "own": ("sbuf", [128, W], "float32"),
    "nei": ("sbuf", [128, W], "float32"),
    "near": ("sbuf", [128, W], "bfloat16"),
    "nq": ("sbuf", [128, NC], CODES),
    "ns": ("sbuf", [128, NC], "uint8"),
    "yo": ("sbuf", [128, W], "float32"),
    "ps": ("psum", [128, 512 * 8], "float32"),
}
SEMAPHORES = ["lb", "la0", "la1", "zero", "hz", "qb", "qa", "sel", "qsel", "selin", "pe", "pu", "act", "max", "vec",
              "near", "qn", "vy0", "vy1", "sty", "nin", "fbin", "tin", "rbin", "rtin", "qh", "sent"]

RELU = ActivationFunctionType.Relu
COPY = ActivationFunctionType.Copy
_PLAN = {}


def _plan(T, topo):
    if _PLAN:
        return _PLAN
    sides = []
    for c in T.cores:
        if topo.host(c) not in sides:
            sides.append(topo.host(c))
    ranks, relays = {}, {}
    mid = [[x for x in range(HOSTS) if x not in sides and topo.rack(x) == topo.rack(sides[1 - s])][0] for s in (0, 1)]
    for s, h in enumerate(sides):
        for k, c in enumerate([c for c in T.cores if topo.host(c) == h]):
            ranks[s, k] = c

            def die(host):
                return [d for d in range(SIM_CORES)
                        if topo.host(d) == host and topo.chip(d) == topo.chip(c) and topo.die(d) == topo.die(c)]
            home = die(h).index(c)
            places = range(len(die(h)))
            apart = max(places, key=lambda n: abs(n - home))
            beside = min([n for n in places if n != apart], key=lambda n: abs(n - apart))
            relays[s, k, 0], relays[s, k, 1] = die(mid[s])[beside], die(mid[s])[home]
            relays[s, k, PLANE] = die(mid[1 - s])[apart]
    _PLAN.update({"rank": ranks, "relay": relays,
                  "role": dict([(c, ("rank",) + sk) for sk, c in ranks.items()]
                               + [(c, ("relay",) + skp) for skp, c in relays.items()])})
    return _PLAN


def _u8(view):
    return view.bitcast(dt.uint8)


def _engines(mask):
    return bin(mask).count("1")


def _halves(mask):
    es = [e for e in range(mask.bit_length()) if mask >> e & 1]
    return [sum(1 << e for e in part) for part in (es[:len(es) // 2], es[len(es) // 2:])]


def _tile(buf, i):
    return buf[:, NC * i:NC * i + NC]


def _pair(buf, n, w=NC):
    return buf[:, 2 * w * n:2 * w * (n + 1)]


def _words(n):
    return slice(HALF * n, HALF * (n + 1))


def _bank(T, n):
    return T.ps[:, 512 * n:512 * n + NC]


def _at(i):
    return slice(W // 2 * (i // 2) + i % 2, W // 2 * (i // 2 + 1), 2)


def _fill(g, T):
    g.vector.memset(T.sel[:], 0.0).then_inc(T.sem.zero, 1)


def _select(g, T, t):
    g.wait_ge(T.sem.zero, 1)
    view = T.sel[:, t:W:4]
    g.affine_select(view, view, [[1, NC]], AluOpType.not_equal, 1.0, 0, -1).then_inc(T.sem.sel, 1)
    g.vector.wait_ge(T.sem.sel, 1)
    g.vector.quantize_mx(_tile(T.selq, t), _tile(T.sels, t), T.sel[:]).then_inc(T.sem.qsel, 1)
    g.wait_ge(T.sem.qsel, 1)


def rank_program(g, core, T, topo):
    plan = _plan(T, topo)
    role = plan["role"].get(core)
    if role is None:
        return
    ranks, relays = plan["rank"], plan["relay"]
    kind, s, k = role[:3]
    sent = [0]

    def send(sem, mask, *pieces):
        moves = []
        for (dst, out, in_), part in zip(pieces, [mask] if len(pieces) == 1 else _halves(mask)):
            rid, pid = topo.addr(dst, core)
            moves.append(RemoteDMATransfer(dst_ids=[DstId(rid=rid, pnc=pid)], dma_engine_mask=part, remote_sem=sem,
                                           src=in_, dst=out))
        g.remote_dma_fused(moves, local_sem=T.sem.sent)
        sent[0] += _engines(mask)

    if kind == "relay":
        _relay(g, core, T, topo, send, ranks[s, k], ranks[1 - s, k], role[3])
    else:
        _rank(g, core, T, topo, send, k, ranks[s, 1 - k], [relays[1 - s, k, part] for part in RELAYS])
    g.wait_ge(T.sem.sent, sent[0])


def _relay(g, core, T, topo, send, near, far, part):
    off = topo.mask(core, near)
    ne = _engines(off)
    user = near if topo.same_plane(core, near) else far
    t, first, last = (1, 0, NC) if part == PLANE else (0, HALF * part, HALF * (part + 1))
    cols = slice(NC * t + first, NC * t + last)
    _fill(g, T)
    _select(g, T, t)
    for view in (_u8(T.selq[:, cols]), T.sels[:, cols]):
        send(T.sem.selin, topo.mask(core, user), (user, view, view))
    if part == PLANE:
        g.wait_ge(T.sem.rbin, ne)
        send(T.sem.fbin, off, (near, T.fbs[:], T.rbs[:]))
        g.wait_ge(T.sem.rtin, ne)
        send(T.sem.tin, off, (near, T.ts[:], T.rts[:]))
    else:
        g.wait_ge(T.sem.rbin, ne // 2)
        send(T.sem.fbin, off, (near, _u8(T.fbq[:, _words(part)]), _u8(T.rbq[:])))
        g.wait_ge(T.sem.rtin, ne)
        send(T.sem.tin, off, (near, _u8(T.tq[:, _words(part)]), _u8(T.rtq[:])))


def _rank(g, core, T, topo, send, k, mate, hops):
    off = topo.mask(core, hops[PLANE])
    ne = _engines(off)
    every = topo.mask(core, mate)
    masks = (every & ~off, every)
    mine = TILES - 2 + k
    v, p = g.vector, g.tensor

    g.sync.dma_start(T.bbf[:], T.b[:]).then_inc(T.sem.lb, 16)
    g.sync.dma_start(_pair(T.abf, 0, W), _pair(T.a, 0, W)).then_inc(T.sem.la0, 16)
    g.sync.wait_ge(T.sem.qb, 1)
    g.sync.dma_start(_pair(T.abf, 1, W), _pair(T.a, 1, W)).then_inc(T.sem.la1, 16)

    _fill(g, T)
    for n in range(2):
        v.memset(T["h%d" % n][:, W // 2:], 0.0).then_inc(T.sem.hz, 1)
    _select(g, T, mine)
    send(T.sem.selin, off, (mate, _u8(_tile(T.selq, mine)), _u8(_tile(T.selq, mine))))

    v.wait_ge(T.sem.lb, 16)
    v.quantize_mx(T.bq[:], T.bs[:], T.bbf[:]).then_inc(T.sem.qb, 1)
    for n in range(2):
        v.wait_ge(T.sem["la%d" % n], 16)
        v.quantize_mx(_pair(T.aq, n), _pair(T.asc, n), _pair(T.abf, n, W)).then_inc(T.sem.qa, 1)

    g.wait_ge(T.sem.qb, 1)
    send(T.sem.rbin, off, *[(hops[n], _u8(T.rbq[:]), _u8(T.bq[:, _words(n)])) for n in range(2)])
    send(T.sem.rbin, off, (hops[PLANE], T.rbs[:], T.bs[:]))
    for n in range(2):
        g.wait_ge(T.sem.qa, n + 1)
        send(T.sem.nin, masks[n], (mate, _u8(_pair(T.noq, n)), _u8(_pair(T.aq, n))))
    send(T.sem.nin, every, (mate, T.nos[:], T.asc[:]))
    send(T.sem.selin, off, (mate, _tile(T.sels, mine), _tile(T.sels, mine)))

    own_b, far_b = (T.bq, T.bs), (T.fbq, T.fbs)
    own_a, nei_a = (T.aq, T.asc), (T.noq, T.nos)
    todo = [(own_a, i, own_b, i, T.own) for i in range(TILES)]
    for n in range(2):
        two = (2 * n, 2 * n + 1)
        todo += [(own_a, i, far_b, 4 + i, T.fo) for i in two] + [(nei_a, i, far_b, i, T.fn) for i in two]
    todo += [(nei_a, i, own_b, 4 + i, T.nei) for i in range(TILES)]
    last = {}
    acts = 0
    counts = {}
    p.wait_ge(T.sem.qb, 1)
    p.wait_ge(T.sem.qa, 2)
    for j, (a, i, b, at, dst) in enumerate(todo):
        if j == TILES:
            p.wait_ge(T.sem.fbin, 3 * ne)
        if dst is T.fn and i == 0:
            p.wait_ge(T.sem.nin, _engines(masks[0]) + _engines(masks[1]) + _engines(every))
        if at in last:
            p.wait_ge(T.sem.act, last[at])
        p.matmul_mx(_bank(T, at), _tile(a[0], i), _tile(a[1], i), b[0][:], b[1][:], True, True).then_inc(T.sem.pe, 1)
        if dst is T.fn and i == 0:
            v.wait_ge(T.sem.pe, j + 1)
            v.tensor_scalar(T.fn[:, _at(i)], _bank(T, at), 0.0, None, AluOpType.max).then_inc(T.sem.max, 1)
            counts[i] = acts
        else:
            g.scalar.wait_ge(T.sem.pe, j + 1)
            g.scalar.activation(dst[:, _at(i)], _bank(T, at), RELU).then_inc(T.sem.act, 1)
            acts += 1
            last[at] = acts
            if dst is T.fn:
                counts[i] = acts
        if dst is T.fn and i % 2 == 1:
            n = i // 2
            if n == 0:
                v.wait_ge(T.sem.hz, 2)
                v.wait_ge(T.sem.max, 1)
            for m in (i - 1, i):
                v.wait_ge(T.sem.act, counts[m])
                v.tensor_tensor(T["h%d" % n][:, m % 2:W // 2:2], T.fo[:, _at(m)], T.fn[:, _at(m)],
                                AluOpType.add).then_inc(T.sem.vec, 1)
            v.wait_ge(T.sem.vec, 2 * (n + 1))
            if n:
                v.wait_ge(T.sem.qh, n)
            words = slice(HALF * n, HALF * n + NC)
            v.quantize_mx(T.hq[:, words], T.hs[:, words], T["h%d" % n][:]).then_inc(T.sem.qh, 1)
            g.wait_ge(T.sem.qh, n + 1)
            send(T.sem.rtin, off, (hops[n], _u8(T.rtq[:]), _u8(T.hq[:, _words(n)])))
    send(T.sem.rtin, off, (hops[PLANE], T.rts[:], T.hs[:, :NC]))
    v.wait_ge(T.sem.act, acts)
    v.tensor_tensor(T.near[:], T.own[:], T.nei[:], AluOpType.add).then_inc(T.sem.near, 1)
    v.wait_ge(T.sem.near, 1)
    v.quantize_mx(T.nq[:], T.ns[:], T.near[:]).then_inc(T.sem.qn, 1)

    p.wait_ge(T.sem.qsel, 1)
    p.wait_ge(T.sem.selin, 8 * ne)
    p.wait_ge(T.sem.act, acts)
    p.wait_ge(T.sem.max, 1)
    p.wait_ge(T.sem.qn, 1)
    for t in range(TILES):
        p.matmul_mx(_bank(T, t), _tile(T.selq, t), _tile(T.sels, t), T.nq[:], T.ns[:], True, False)
    p.wait_ge(T.sem.tin, 3 * ne)
    for t in range(TILES):
        p.matmul_mx(_bank(T, t), _tile(T.selq, t), _tile(T.sels, t), T.tq[:], T.ts[:], False,
                    True).then_inc(T.sem.pu, 1)
    for t in range(TILES):
        q = g.scalar if t % 2 else v
        q.wait_ge(T.sem.pu, t + 1)
        for half in range(2):
            for n in range(2):
                y0 = W // 2 * half + 4 * (t // 2) + 2 * n + t % 2
                x0 = 512 * t + HALF * n + HALF // 2 * half
                to, of = T.yo[:, y0:W // 2 * (half + 1):8], T.ps[:, x0:x0 + HALF // 2]
                (q.activation(to, of, COPY) if t % 2 else q.tensor_copy(to, of)).then_inc(T.sem["vy%d" % half], 1)
    for half in range(2):
        cols = slice(W // 2 * half, W // 2 * (half + 1))
        g.sync.wait_ge(T.sem["vy%d" % half], 8)
        g.sync.dma_start(T.y[:, cols], T.yo[:, cols]).then_inc(T.sem.sty, 16)
    g.sync.wait_ge(T.sem.sty, 32)
